import numpy as np, ml_dtypes
CORES = [78,86,94,102,110,118]
N = 6
BF = ml_dtypes.bfloat16
X, Y, n, ORD = 48, 128, 32, 4
def normal(rng, *shape):
    v = rng.standard_normal(shape, dtype=np.float32)
    return np.where(v < 0, np.float32(-1), np.float32(1)) * np.clip(np.abs(v), np.float32(2.0 ** -8), np.float32(3))
def setup_inputs(rng):
    q = normal(rng, N, 128, n) * np.exp2(rng.integers(-1, 2, (N, 128, 1))).astype(np.float32)
    refl = ((0.5 + rng.random((N, 128, n))) * 2.0 ** -4 * rng.choice(np.array([-1.0, 1.0]), (N, 128, n))).astype(np.float32)
    return {"px": rng.integers(0, X, (N, 8, n)).astype(np.int32), "py": rng.integers(0, Y, (N, 8, n)).astype(np.int32), "q": q.astype(np.float32), "refl": refl,
            "green": normal(rng, N, 128, X * Y).astype(BF)}
def setup_inputs_corners(rng):
    d = setup_inputs(rng)
    d["px"] = rng.choice(np.array([0, 1, X - 2, X - 1]), (N, 8, n)).astype(np.int32); d["py"] = rng.choice(np.array([0, 1, Y - 2, Y - 1]), (N, 8, n)).astype(np.int32)
    d["px"][:, :, 0] = 0; d["py"][:, :, 0] = 0; d["px"][:, :, n - 1] = X - 1; d["py"][:, :, n - 1] = Y - 1; return d
def setup_inputs_lines(rng):
    d = setup_inputs(rng)
    for g in range(8):
        if g % 2 == 0: d["px"][:, g] = rng.integers(0, X)
        else: d["py"][:, g] = rng.integers(0, Y)
    return d
def setup_inputs_heap(rng):
    d = setup_inputs(rng)
    for g in range(8):
        r = int(rng.integers(0, N)); t = (r + 1 + int(rng.integers(0, N - 1))) % N; u = (t + 1) % N
        if u == r: u = (u + 1) % N
        d["px"][r, g] = rng.integers(0, X); d["py"][r, g] = rng.integers(0, Y)
        d["px"][t, g] = d["px"][u, g]; d["py"][t, g] = d["py"][u, g]
    return d
def setup_inputs_lamp(rng):
    d = setup_inputs(rng); keep = np.zeros((N, 8), np.float32); keep[rng.integers(0, N, 8), np.arange(8)] = 1
    d["q"] = d["q"] * np.repeat(keep, 16, axis=1)[:, :, None]; d["refl"] = d["refl"] * (rng.random((N, 1, n)) < 0.5).astype(np.float32); return d
def setup_inputs_spread(rng):
    d = setup_inputs(rng); z = np.exp2(rng.integers(-6, 7, (N, 1, n))) * (rng.random((N, 1, n)) > 0.0625)
    d["q"] = (d["q"] * z).astype(np.float32); d["refl"] = d["refl"] * np.float32(2.0 ** -5)
    c = (np.exp2(rng.integers(-6, 7, (N, 1, X * Y))) * (rng.random((N, 1, X * Y)) > 0.0625)).astype(np.float32); s = np.exp2(rng.integers(-2, 2, (N, 128, 1))).astype(np.float32)
    d["green"] = (d["green"].astype(np.float32) * s * c).astype(BF); return d
def check_inputs(d):
    bad = []
    if not ((d["px"] >= 0) & (d["px"] < X)).all(): bad.append("px_range")
    if not ((d["py"] >= 0) & (d["py"] < Y)).all(): bad.append("py_range")
    for k in ("q", "refl", "green"):
        if not np.isfinite(d[k].astype(np.float32)).all(): bad.append(k + "_finite")
    return bad
def reference(px, py, q, refl, green):
    y = np.zeros((N, 128, n), np.float64); own = np.arange(n)
    for g in range(8):
        p = slice(16 * g, 16 * g + 16)
        cx = px[:, g].astype(np.int64).reshape(-1); cy = py[:, g].astype(np.int64).reshape(-1)
        off = np.abs(cx[:, None] - cx[None, :]) * Y + np.abs(cy[:, None] - cy[None, :])
        parts = []
        for s in range(N):
            m = green[s, p].astype(np.float64)[:, off[:, s * n:(s + 1) * n]]; m[:, s * n + own, own] = 0
            parts.append(m)
        M = np.concatenate(parts, axis=2)
        w = q[:, p].astype(np.float64).transpose(1, 0, 2).reshape(16, N * n); a = refl[:, p].astype(np.float64).transpose(1, 0, 2).reshape(16, N * n)
        total = np.zeros((16, N * n), np.float64)
        for o in range(ORD):
            fd = np.matmul(M, w[:, :, None])[:, :, 0]
            total = total + fd; w = a * fd
        y[:, p] = total.reshape(16, N, n).transpose(1, 0, 2)
    return {"y": y.astype(np.float32)}

@@ -1,0 +1,345 @@
+from concourse.bass import DstId, RemoteDMATransfer
+from concourse.mybir import AluOpType, AxisListType, ActivationFunctionType
+
+NR, NS, ORD, TAB = 6, 32, 4, 6144
+NLOC = 125
+
+SCRATCH = {
+    "PXY": ("sbuf", [128, 2, 32], "int32"),
+    "PB": ("sbuf", [128, 2, 32], "bfloat16"),
+    "P": ("sbuf", [128, 6, 2, 32], "bfloat16"),
+    "GR": ("sbuf", [128, TAB], "bfloat16"),
+    "G": ("sbuf", [128, 6144], "bfloat16"),
+    "Mt": ("sbuf", [128, 6144], "bfloat16"),
+    "OFF": ("sbuf", [128, 384], "uint16"),
+    "AB": ("sbuf", [128, 4, 6, 32], "bfloat16"),
+    "SELI": ("sbuf", [128, 128], "float32"),
+    "SEL": ("sbuf", [128, 128], "bfloat16"),
+    "D": ("sbuf", [128, 128], "float32"),
+    "ID": ("sbuf", [128, 128], "bfloat16"),
+    "S2": ("sbuf", [128, 64], "float32"),
+    "T64": ("sbuf", [128, 64], "float32"),
+    "T32": ("sbuf", [128, 32], "float32"),
+    "M16": ("sbuf", [128, 16], "float32"),
+    "MK": ("sbuf", [128, 64], "float32"),
+    "TMP": ("sbuf", [128, 64], "float32"),
+    "OWN": ("sbuf", [128, 4], "float32"),
+    "PAR": ("sbuf", [128, 4], "float32"),
+    "SM": ("sbuf", [128, 96], "float32"),
+    "Wb": ("sbuf", [128, 4, 96], "bfloat16"),
+    "Wp": ("sbuf", [128, 96], "bfloat16"),
+    "E0": ("sbuf", [128, 4, 96], "float32"),
+    "E1": ("sbuf", [128, 4, 96], "float32"),
+    "E2": ("sbuf", [128, 4, 96], "float32"),
+    "Sb": ("sbuf", [128, ORD, 192], "float32"),
+    "L": ("sbuf", [128, ORD, 160], "float32"),
+    "Q": ("sbuf", [128, 32], "float32"),
+    "QT": ("sbuf", [128, 32], "float32"),
+    "RF": ("sbuf", [128, 32], "float32"),
+    "RN": ("sbuf", [128, 32], "float32"),
+    "RT": ("sbuf", [128, 32], "float32"),
+    "W": ("sbuf", [128, 32], "float32"),
+    "R": ("sbuf", [128, 32], "float32"),
+    "U": ("sbuf", [128, 32], "float32"),
+    "Z": ("sbuf", [128, 32], "float32"),
+    "A0": ("sbuf", [128, 32], "float32"),
+    "A1": ("sbuf", [128, 32], "float32"),
+    "A2": ("sbuf", [128, 32], "float32"),
+    "F": ("sbuf", [128, ORD, 32], "float32"),
+    "YA": ("sbuf", [128, 32], "float32"),
+    "YB": ("sbuf", [128, 32], "float32"),
+    "YN": ("sbuf", [128, 32], "float32"),
+    "PR0": ("psum", [128, 4, 128], "float32"),
+    "PR1": ("psum", [128, 4, 128], "float32"),
+    "PR2": ("psum", [128, 4, 128], "float32"),
+    "PR3": ("psum", [128, 4, 128], "float32"),
+    "PT0": ("psum", [128, 8, 2, 32], "float32"),
+    "PT1": ("psum", [128, 8, 2, 32], "float32"),
+    "PT2": ("psum", [128, 8, 2, 32], "float32"),
+    "PI0": ("psum", [128, 8, 2, 32], "float32"),
+}
+SEMAPHORES = (["sent"] + ["arr%d_%d" % (o, k) for o in range(ORD + 1) for k in range(3)]
+              + ["s%d" % k for k in range(NLOC)])
+
+GROUPS = ((0, 1), (2, 3), (4,))
+
+
+def rank_program(g, core, T, topo):
+    rank = T.rank_of(core)
+    if rank is None:
+        return
+    cores = list(T.cores)
+    A, ACT = AluOpType, ActivationFunctionType
+    V, S, PE = g.vector, g.scalar, g.tensor
+    queue = {"g": g, "v": V, "s": S, "p": PE, "y": g.sync}
+
+    def hops(a, b):
+        ca, cb = topo.chip(a), topo.chip(b)
+        return 0 if ca == cb else (1 if topo.mates(ca, cb) or topo.same_plane(ca, cb) else 2)
+    dist = sorted(range(1, NR), key=lambda d: (-sum(hops(cores[r], cores[(r + d) % NR]) for r in range(NR)), d))
+
+    cnt, waited, site, res = {}, {}, {}, {}
+    know = {q: {} for q in queue}
+
+    def need(q, ev):
+        name, n, kn = ev
+        if know[q].get(name, 0) >= n:
+            return
+        queue[q].wait_ge(T.sem[name], n)
+        waited[name] = max(waited.get(name, 0), n)
+        know[q][name] = n
+        for k, v in kn.items():
+            if know[q].get(k, 0) < v:
+                know[q][k] = v
+
+    def before(q, reads, writes):
+        evs = []
+        for r in reads:
+            evs += res.setdefault(r, [[], []])[0]
+        for w in writes:
+            e = res.setdefault(w, [[], []])
+            evs += e[0] + e[1]
+        for ev in reversed(evs):
+            need(q, ev)
+
+    def op(q, fns, reads, writes, name=None, inc=1):
+        before(q, reads, writes)
+        if name is None:
+            name = "once%d" % len(site)
+        if name not in site:
+            site[name] = "s%d" % len(site)
+        sem = site[name]
+        for fn in fns:
+            fn().then_inc(T.sem[sem], inc)
+            cnt[sem] = cnt.get(sem, 0) + inc
+        ev = (sem, cnt[sem], dict(know[q]))
+        for r in reads:
+            res[r][1].append(ev)
+        for w in writes:
+            res[w] = [[ev], []]
+
+    def send(rnd, k, srcs, dsts, peers, reads):
+        before("g", reads, [])
+        sem = T.sem["arr%d_%d" % (rnd, k)]
+        trs, total = [], 0
+        for n, peer in enumerate(peers):
+            eng = topo.engines(core, peer)
+            share = len(eng) // len(peers)
+            m = sum(1 << e for e in eng[n * share:(n + 1) * share])
+            rid, pid = topo.addr(peer)[0:2]
+            total += share
+            if len(peers) == 1:
+                g.remote_dma(dsts[n], srcs[n], sem, T.sem["sent"], pid, rid, m)
+            else:
+                trs.append(RemoteDMATransfer(dst_ids=[DstId(rid=rid, pnc=pid)], dma_engine_mask=m, remote_sem=sem,
+                                             src=srcs[n], dst=dsts[n]))
+        if trs:
+            g.remote_dma_fused(trs, local_sem=T.sem["sent"])
+        cnt["sent"] = cnt.get("sent", 0) + total
+
+    for rnd in range(ORD + 1):
+        for k, slots in enumerate(GROUPS):
+            sign = 1 if rnd == 0 else -1
+            n = sum(len(topo.engines(cores[(rank + sign * dist[s]) % NR], core)) // len(slots) for s in slots)
+            name = "arr%d_%d" % (rnd, k)
+            cnt[name] = n
+            res[name] = [[(name, n, {})], []]
+
+    tt = V.tensor_tensor
+
+    op("y", [lambda: g.sync.dma_start(T.PXY[0:8, 0, :], T.px[:])], [], ["px"], inc=16)
+    op("s", [lambda: S.dma_start(T.PXY[0:8, 1, :], T.py[:])], [], ["py"], inc=16)
+    op("y", [lambda: g.sync.dma_start(T.GR[:], T.green[:])], [], ["GR"], inc=16)
+    op("s", [lambda: S.dma_start(T.Q[:], T.q[:])], [], ["Q"], inc=16)
+    op("y", [lambda: g.sync.dma_start(T.RF[:], T.refl[:])], [], ["RF"], inc=16)
+
+    op("g", [lambda: g.iota(T.SELI[0:8, :], [[1, 8], [0, 16]], 0, -1, allow_small_or_imprecise_dtypes=True)], [], ["SELI"])
+    op("g", [lambda: g.iota(T.D[:], [[1, 128]], 0, -1, allow_small_or_imprecise_dtypes=True)], [], ["D"])
+    op("v", [lambda: V.memset(T.Wb[:], 0.0)], [], ["WbV", "WbS"])
+    op("v", [lambda: V.memset(T.SM[:], 0.0)], [], ["SM"])
+    op("v", [lambda: V.tensor_scalar(T.SEL[0:8, :], T.SELI[0:8, :], 0.0, None, A.is_equal)], ["SELI"], ["SEL"])
+    op("v", [lambda: V.tensor_scalar(T.ID[:], T.D[:], 0.0, None, A.is_equal)], ["D"], ["ID"])
+    op("v", [lambda: tt(T.T64[:], T.ID[:, 0:64], T.ID[:, 64:128], A.add)], ["ID"], ["T64"])
+    op("v", [lambda: tt(T.T32[:], T.T64[:, 0:32], T.T64[:, 32:64], A.add)], ["T64"], ["T32"])
+    op("v", [lambda: tt(T.M16[:], T.T32[:, 0:16], T.T32[:, 16:32], A.add)], ["T32"], ["M16"])
+    op("v", [lambda: V.tensor_copy(T.PB[0:8, :, :], T.PXY[0:8, :, :])], ["px", "py"], ["PB"])
+    op("p", [lambda: PE.matmul(T.PI0[:, 0, :, :], T.SEL[0:8, :], T.PB[0:8, :, :], True, True)], ["SEL", "PB"], ["PI0"])
+    op("v", [lambda: V.tensor_copy(T.P[:, 5, :, :], T.PI0[:, 0, :, :])], [], ["PI0", "Pown"])
+    for k, slots in enumerate(GROUPS):
+        send(0, k, [T.P[:, 5, :, :] for s in slots], [T.P[:, s, :, :] for s in slots],
+             [cores[(rank - dist[s]) % NR] for s in slots], ["Pown"])
+
+    op("v", [lambda c=c: V.tensor_scalar(T.MK[:, 16 * c:16 * c + 16], T.M16[:], -128.0 if c < 2 else -1.0, None, A.mult)
+             for c in range(4)], ["M16"], ["MK"])
+    op("v", [lambda: tt(T.TMP[:], T.P[:, 5, :, :], T.MK[:], A.mult)], ["Pown", "MK"], ["TMP"])
+    op("v", [lambda c=c: V.tensor_reduce(T.OWN[:, c:c + 1], T.TMP[:, 16 * c:16 * c + 16], AxisListType.X, A.add)
+             for c in range(4)], ["TMP"], ["OWN"])
+
+    def offsets_s(a, b, src):
+        op("s", [lambda c=c: S.activation(T.AB[:, c, a:b, :], T.P[:, a:b, c // 2, :], ACT.Abs, bias=T.OWN[:, c:c + 1],
+                                          scale=128.0 if c < 2 else 1.0) for c in range(4)], ["OWN", src], ["AB%d" % a])
+
+    def offsets_p(a, b, bank):
+        fns = []
+        for h in range(2):
+            fns.append(lambda h=h: PE.matmul(T[bank][:, h, 0:b - a, :], T.ID[:], T.AB[:, h, a:b, :], True, False))
+            fns.append(lambda h=h: PE.matmul(T[bank][:, h, 0:b - a, :], T.ID[:], T.AB[:, 2 + h, a:b, :], False, True))
+        op("p", fns, ["ID", "AB%d" % a], [bank])
+
+    def offsets_v(a, b, bank):
+        op("v", [lambda h=h: V.tensor_copy(T.OFF[:, 64 * a + h:64 * b:2], T[bank][:, h, 0:b - a, :]) for h in range(2)],
+           [], [bank] + ["OFF%d" % s for s in range(a, b)])
+
+    def gather(q, n):
+        src = lambda: T.GR[:, 0:TAB].indirect(T.OFF[:, 32 * n:32 * n + 32])
+        out = T.G[:, 512 * n:512 * n + 512]
+        fn = (lambda: V.tensor_copy(out, src())) if q == "v" else (lambda: S.activation(out, src(), ACT.Copy))
+        op(q, [fn], ["GR", "OFF%d" % (n // 2)], ["G%d" % n])
+
+    def turn(n, m=1):
+        op("v", [lambda: V.transpose(T.Mt[:, 512 * n:512 * (n + m)], T.G[:, 512 * n:512 * (n + m)])],
+           ["G%d" % x for x in range(n, n + m)], ["Mt%d" % x for x in range(n, n + m)])
+
+    def lay(dst, dkey, mid, mkey, src, skey):
+        op("v", [lambda: V.transpose(mid[:], src[:])], [skey], [mkey])
+        op("v", [lambda ab=ab: V.tensor_copy(dst[:, ab:32:2], mid[:, 16 * ab:16 * ab + 16]) for ab in range(2)], [mkey], [dkey])
+
+    def split_tail():
+        hi, mid, lo = T.Wp[:, 0:96:3], T.Wp[:, 1:96:3], T.Wp[:, 2:96:3]
+        op("v", [lambda: tt(T.R[:], T.W[:], hi, A.subtract), lambda: tt(mid, T.W[:], hi, A.subtract)],
+           ["W", "hi"], ["R", "mid"], "sp1")
+        op("v", [lambda: tt(lo, T.R[:], mid, A.subtract)], ["R", "mid"], ["lo"], "sp2")
+        op("s", [lambda b=b: S.activation(T.Wb[32 * b:32 * b + 32, b, :], T.Wp[32 * b:32 * b + 32, :], ACT.Copy)
+                 for b in (2, 3)], ["hi", "mid", "lo"], ["WbS"], "plS")
+        op("v", [lambda b=b: V.tensor_copy(T.Wb[32 * b:32 * b + 32, b, :], T.Wp[32 * b:32 * b + 32, :])
+                 for b in (0, 1)], ["hi", "mid", "lo"], ["WbV"], "plV")
+
+    def mm(k, bank=None, c0=0, c1=16):
+        bank = k if bank is None else bank
+        op("p", [lambda c=c: PE.matmul(T["PR%d" % bank][:, :, 6 * c:6 * c + 6], T.Mt[:, 2048 * k + c:2048 * k + 2048:16],
+                                       T.Wb[:, :, 6 * c:6 * c + 6], True, True) for c in range(c0, c1)],
+           ["WbS", "WbV"] + ["Mt%d" % x for x in range(4 * k, 4 * k + 4)], ["PR%d" % bank], "mm%d" % bank)
+
+    def scan(k, bank=None, c0=0, c1=16):
+        bank = k if bank is None else bank
+        keys = ["E%d_%d" % (k, h) for h in range(c0 // 8, c1 // 8)]
+        op("v", [lambda b=b: V.tensor_tensor_scan(T["E%d" % k][:, b, 6 * c0:6 * c1], T["PR%d" % bank][:, b, 6 * c0:6 * c1],
+                                                  T.SM[:, 6 * c0:6 * c1], 0.0, A.add, A.mult) for b in range(4)],
+           ["SM"], ["PR%d" % bank] + keys, "scan%d" % bank)
+
+    def back(k):
+        op("p", [lambda: PE.matmul(T["PT%d" % k][:, 0, :, :], T["E%d" % k][:, :, 2:96:3], T.S2[:], True, True)],
+           ["E%d_0" % k, "E%d_1" % k, "S2"], ["PT%d" % k], "back%d" % k)
+
+    def out(o, k):
+        key = "Sb%d_%d" % (o, k)
+        op("v", [lambda: V.transpose(T.Sb[:, o, 64 * k:64 * k + 64], T["PT%d" % k][:, 0, :, :])], [], ["PT%d" % k, key], "out%d" % k)
+        slots = GROUPS[k]
+        send(o + 1, k, [T.Sb[:, o, 32 * s:32 * s + 32] for s in slots], [T.L[:, o, 32 * s:32 * s + 32] for s in slots],
+             [cores[(rank + dist[s]) % NR] for s in slots], [key])
+
+    def receive(o):
+        land = lambda s: T.L[:, o, 32 * s:32 * s + 32]
+        own, ownkey = T.Sb[:, o, 160:192], "Sb%d_2" % o
+        if o == ORD - 1:
+            op("v", [lambda: tt(T.A0[:], own, T.YB[:], A.add)], [ownkey, "YB"], ["A0"])
+            own, ownkey = T.A0[:], "A0"
+        op("v", [lambda: tt(T.U[:], land(0), land(1), A.add)], ["arr%d_0" % (o + 1)], ["U"], "u")
+        op("v", [lambda: tt(T.A1[:], T.U[:], own, A.add)], ["U", ownkey], ["A1"], "a1")
+        op("v", [lambda: tt(T.Z[:], land(2), land(3), A.add)], ["arr%d_1" % (o + 1)], ["Z"], "z")
+        op("v", [lambda: tt(T.A2[:], T.A1[:], T.Z[:], A.add)], ["A1", "Z"], ["A2"], "a2")
+        if o == ORD - 1:
+            op("v", [lambda ab=ab: tt(T.F[:, o, 16 * ab:16 * ab + 16], T.A2[:, ab:32:2], T.L[:, o, 128 + ab:160:2], A.add)
+                     for ab in range(2)], ["A2", "arr%d_2" % (o + 1)], ["F%d" % o])
+            op("v", [lambda: V.transpose(T.YN[:], T.F[:, o, :])], ["F%d" % o], ["YN"])
+            op("y", [lambda: g.sync.dma_start(T.y[:], T.YN[:])], ["YN"], ["y"], inc=16)
+            return
+        op("v", [lambda: tt(T.F[:, o, :], T.A2[:], land(4), A.add)], ["A2", "arr%d_2" % (o + 1)], ["F%d" % o], "f")
+        op("v", [lambda: tt(T.Wp[:, 0:96:3], T.F[:, o, :], T.RT[:], A.mult), lambda: tt(T.W[:], T.F[:, o, :], T.RT[:], A.mult)],
+           ["F%d" % o, "RT"], ["W", "hi"], "sp0")
+        split_tail()
+        if o == 1:
+            op("v", [lambda: tt(T.YA[:], T.F[:, 0, :], T.F[:, 1, :], A.add)], ["F0", "F1"], ["YA"])
+        if o == 2:
+            op("v", [lambda: tt(T.YB[:], T.YA[:], T.F[:, 2, :], A.add)], ["YA", "F2"], ["YB"])
+
+    offsets_s(5, 6, "Pown")
+    offsets_p(5, 6, "PT2")
+    op("v", [lambda: tt(T.S2[:], T.ID[:, 0:128:2], T.ID[:, 1:128:2], A.add)], ["ID"], ["S2"])
+    op("v", [lambda: V.tensor_reduce(T.PAR[:, 0:1], T.M16[:, 0:16:2], AxisListType.X, A.add),
+             lambda: V.tensor_reduce(T.PAR[:, 1:2], T.M16[:, 1:16:2], AxisListType.X, A.add)], ["M16"], ["PAR"])
+    offsets_v(5, 6, "PT2")
+    op("v", [lambda c=c: V.tensor_scalar(T.SM[:, c:96:6], T.SM[:, c:96:6], T.PAR[:, c // 3:c // 3 + 1], None, A.add)
+             for c in range(6)], ["PAR"], ["SM"])
+    lay(T.W, "W", T.QT, "QT", T.Q, "Q")
+    op("v", [lambda: V.tensor_copy(T.Wp[:, 0:96:3], T.W[:])], ["W"], ["hi"])
+    split_tail()
+
+    gather("s", 10)
+    gather("v", 11)
+    op("v", [lambda: V.memset(T.G[:, 5120:6144:33], 0.0)], [], ["G10", "G11"])
+    turn(10, 2)
+    offsets_s(0, 2, "arr0_0")
+    offsets_p(0, 2, "PI0")
+    offsets_v(0, 2, "PI0")
+    gather("s", 0)
+    gather("v", 3)
+    offsets_s(2, 4, "arr0_1")
+    offsets_p(2, 4, "PT2")
+    gather("s", 1)
+    offsets_s(4, 5, "arr0_2")
+    offsets_p(4, 5, "PI0")
+    turn(3)
+    turn(0)
+    offsets_v(2, 4, "PT2")
+    gather("v", 7)
+    gather("s", 2)
+    gather("s", 4)
+    turn(1)
+    offsets_v(4, 5, "PI0")
+    turn(7)
+    turn(2)
+    mm(0)
+    gather("s", 5)
+    gather("s", 6)
+    gather("s", 8)
+    gather("v", 9)
+    scan(0)
+    back(0)
+    turn(4)
+    out(0, 0)
+    turn(5)
+    turn(9)
+    turn(6)
+    mm(1)
+    scan(1)
+    back(1)
+    turn(8)
+    mm(2)
+    out(0, 1)
+    scan(2)
+    back(2)
+    out(0, 2)
+    lay(T.RT, "RT", T.RN, "RN", T.RF, "RF")
+    receive(0)
+
+    for o in range(1, ORD):
+        mm(0, 0, 0, 8)
+        mm(0, 3, 8, 16)
+        mm(1)
+        scan(0, 0, 0, 8)
+        scan(0, 3, 8, 16)
+        back(0)
+        mm(2)
+        out(o, 0)
+        scan(1)
+        back(1)
+        scan(2)
+        back(2)
+        out(o, 1)
+        out(o, 2)
+        receive(o)
+
+    for name, n in cnt.items():
+        if waited.get(name, 0) < n:
+            g.wait_ge(T.sem[name], n)

@@ -2,35 +2,54 @@ from concourse.bass import DstId, RemoteDMATransfer
 from concourse.mybir import AluOpType, AxisListType, ActivationFunctionType
 
 NR, NS, ORD, TAB = 6, 32, 4, 6144
-NLOC = 125
+OWN_SLOT = NR - 1
+NLOC = 120
+L3, L4 = ((0, 1), (2, 3), (4, 5)), ((0, 1), (2, 3), (4,), (5,))
+CFG = {
+    "split": 0,
+    "o1": (L4, "A0,2,0 S20,21 V21,22 C0,2,0 A2,5,1 V6,8 S0,2 C2,5,1 t6,8 S2,4 t0,2 V14,16 S4,6 t2,4 t14,16 S8,10 t4,6 m0 "
+               "V18,20 S10,12 s0 b0 t8,10 o0 S12,14 t18,20 t10,12 S16,17 t20,22 S17,18 t12,14 m1 t16,17 S22,24 t17,18 m2 "
+               "s1 b1 s2 b2 o1 t22,24 m3 o2 r1 s3 b3 r2 o3 +u,0,1 +z,2,3 +w,u,5 +x,w,z fx,4"),
+    "mid": (L3, "m0 m1 m2a s0 b0 m2b s1 b1 o0 s2a o1 s2b b2 y1 o2 +u,0,1 +w,u,5 +z,2,3 +x,w,z fx,4"),
+    "last": (L3, "m0 m1 m2a s0 b0 m2b s1 b1 o0 s2a o1 s2b b2 y1 o2 y2 +u,0,1 +v,u,Y +w,v,5 +z,2,3 +x,w,z fx,4"),
+}
 
 SCRATCH = {
     "PXY": ("sbuf", [128, 2, 32], "int32"),
     "PB": ("sbuf", [128, 2, 32], "bfloat16"),
     "P": ("sbuf", [128, 6, 2, 32], "bfloat16"),
-    "GR": ("sbuf", [128, TAB], "bfloat16"),
+    "GR": ("sbuf", [128, TAB + 16], "bfloat16"),
     "G": ("sbuf", [128, 6144], "bfloat16"),
     "Mt": ("sbuf", [128, 6144], "bfloat16"),
     "OFF": ("sbuf", [128, 384], "uint16"),
     "AB": ("sbuf", [128, 4, 6, 32], "bfloat16"),
+    "DG": ("sbuf", [128, 2, 32], "bfloat16"),
     "SELI": ("sbuf", [128, 128], "float32"),
     "SEL": ("sbuf", [128, 128], "bfloat16"),
     "D": ("sbuf", [128, 128], "float32"),
     "ID": ("sbuf", [128, 128], "bfloat16"),
     "S2": ("sbuf", [128, 64], "float32"),
-    "T64": ("sbuf", [128, 64], "float32"),
-    "T32": ("sbuf", [128, 32], "float32"),
+    "S4": ("sbuf", [128, 32], "float32"),
+    "IM": ("sbuf", [128, 8, 16], "float32"),
     "M16": ("sbuf", [128, 16], "float32"),
     "MK": ("sbuf", [128, 64], "float32"),
     "TMP": ("sbuf", [128, 64], "float32"),
     "OWN": ("sbuf", [128, 4], "float32"),
-    "PAR": ("sbuf", [128, 4], "float32"),
-    "SM": ("sbuf", [128, 96], "float32"),
-    "Wb": ("sbuf", [128, 4, 96], "bfloat16"),
-    "Wp": ("sbuf", [128, 96], "bfloat16"),
+    "PC": ("sbuf", [128, 8], "int32"),
+    "PCI": ("sbuf", [128, 8], "int32"),
+    "PCF": ("sbuf", [128, 8], "float32"),
+    "I16": ("sbuf", [128, 64], "float32"),
+    "I2": ("sbuf", [128, 96], "float32"),
+    "I4": ("sbuf", [128, 96], "float32"),
+    "SM2": ("sbuf", [128, 96], "float32"),
+    "SM4": ("sbuf", [128, 96], "float32"),
+    "Wb": ("sbuf", [128, 4, 32, 3], "bfloat16"),
+    "Wp": ("sbuf", [128, 32, 2], "bfloat16"),
     "E0": ("sbuf", [128, 4, 96], "float32"),
     "E1": ("sbuf", [128, 4, 96], "float32"),
     "E2": ("sbuf", [128, 4, 96], "float32"),
+    "E3": ("sbuf", [128, 4, 96], "float32"),
+    "AR": ("sbuf", [128, 32], "float32"),
     "Sb": ("sbuf", [128, ORD, 192], "float32"),
     "L": ("sbuf", [128, ORD, 160], "float32"),
     "Q": ("sbuf", [128, 32], "float32"),
@@ -40,11 +59,7 @@ SCRATCH = {
     "RT": ("sbuf", [128, 32], "float32"),
     "W": ("sbuf", [128, 32], "float32"),
     "R": ("sbuf", [128, 32], "float32"),
-    "U": ("sbuf", [128, 32], "float32"),
-    "Z": ("sbuf", [128, 32], "float32"),
-    "A0": ("sbuf", [128, 32], "float32"),
-    "A1": ("sbuf", [128, 32], "float32"),
-    "A2": ("sbuf", [128, 32], "float32"),
+    "AC": ("sbuf", [128, 6, 32], "float32"),
     "F": ("sbuf", [128, ORD, 32], "float32"),
     "YA": ("sbuf", [128, 32], "float32"),
     "YB": ("sbuf", [128, 32], "float32"),
@@ -53,15 +68,13 @@ SCRATCH = {
     "PR1": ("psum", [128, 4, 128], "float32"),
     "PR2": ("psum", [128, 4, 128], "float32"),
     "PR3": ("psum", [128, 4, 128], "float32"),
-    "PT0": ("psum", [128, 8, 2, 32], "float32"),
-    "PT1": ("psum", [128, 8, 2, 32], "float32"),
-    "PT2": ("psum", [128, 8, 2, 32], "float32"),
-    "PI0": ("psum", [128, 8, 2, 32], "float32"),
+    "PT0": ("psum", [128, 512], "float32"),
+    "PT1": ("psum", [128, 512], "float32"),
+    "PT2": ("psum", [128, 512], "float32"),
+    "PT3": ("psum", [128, 512], "float32"),
 }
-SEMAPHORES = (["sent"] + ["arr%d_%d" % (o, k) for o in range(ORD + 1) for k in range(3)]
+SEMAPHORES = (["sent", "go"] + ["arr%d_%d" % (o, k) for o in range(ORD + 1) for k in range(NR - 1)]
               + ["s%d" % k for k in range(NLOC)])
-
-GROUPS = ((0, 1), (2, 3), (4,))
 
 
 def rank_program(g, core, T, topo):
@@ -118,227 +131,244 @@ def rank_program(g, core, T, topo):
         for w in writes:
             res[w] = [[ev], []]
 
-    def send(rnd, k, srcs, dsts, peers, reads):
+    def send(rnd, slots, reads):
         before("g", reads, [])
-        sem = T.sem["arr%d_%d" % (rnd, k)]
-        trs, total = [], 0
-        for n, peer in enumerate(peers):
+        trs = []
+        for n, s in enumerate(slots):
+            name = "arr%d_%d" % (rnd, s)
+            ahead, behind = cores[(rank + dist[s]) % NR], cores[(rank - dist[s]) % NR]
+            if rnd == 0:
+                peer, sender, src, dst = behind, ahead, T.P[:, OWN_SLOT, :, :], T.P[:, s, :, :]
+            else:
+                peer, sender = ahead, behind
+                src, dst = T.Sb[:, rnd - 1, 32 * s:32 * s + 32], T.L[:, rnd - 1, 32 * s:32 * s + 32]
             eng = topo.engines(core, peer)
-            share = len(eng) // len(peers)
+            share = len(eng) // len(slots)
             m = sum(1 << e for e in eng[n * share:(n + 1) * share])
             rid, pid = topo.addr(peer)[0:2]
-            total += share
-            if len(peers) == 1:
-                g.remote_dma(dsts[n], srcs[n], sem, T.sem["sent"], pid, rid, m)
+            cnt["sent"] = cnt.get("sent", 0) + share
+            cnt[name] = len(topo.engines(sender, core)) // len(slots)
+            res[name] = [[(name, cnt[name], {})], []]
+            if len(slots) == 1:
+                g.remote_dma(dst, src, T.sem[name], T.sem["sent"], pid, rid, m)
             else:
-                trs.append(RemoteDMATransfer(dst_ids=[DstId(rid=rid, pnc=pid)], dma_engine_mask=m, remote_sem=sem,
-                                             src=srcs[n], dst=dsts[n]))
+                trs.append(RemoteDMATransfer(dst_ids=[DstId(rid=rid, pnc=pid)], dma_engine_mask=m, remote_sem=T.sem[name],
+                                             src=src, dst=dst))
         if trs:
             g.remote_dma_fused(trs, local_sem=T.sem["sent"])
-        cnt["sent"] = cnt.get("sent", 0) + total
 
-    for rnd in range(ORD + 1):
-        for k, slots in enumerate(GROUPS):
-            sign = 1 if rnd == 0 else -1
-            n = sum(len(topo.engines(cores[(rank + sign * dist[s]) % NR], core)) // len(slots) for s in slots)
-            name = "arr%d_%d" % (rnd, k)
-            cnt[name] = n
-            res[name] = [[(name, n, {})], []]
+    tt, ts = V.tensor_tensor, V.tensor_scalar
 
-    tt = V.tensor_tensor
+    def iota(out, key, pattern, mult):
+        op("g", [lambda: g.iota(out, pattern, 0, mult, allow_small_or_imprecise_dtypes=True)], [], [key])
 
+    cut = CFG["split"] or TAB
     op("y", [lambda: g.sync.dma_start(T.PXY[0:8, 0, :], T.px[:])], [], ["px"], inc=16)
     op("s", [lambda: S.dma_start(T.PXY[0:8, 1, :], T.py[:])], [], ["py"], inc=16)
-    op("y", [lambda: g.sync.dma_start(T.GR[:], T.green[:])], [], ["GR"], inc=16)
+    op("y", [lambda: g.sync.dma_start(T.GR[:, 0:cut], T.green[:, 0:cut])], [], ["GR0"], inc=16)
     op("s", [lambda: S.dma_start(T.Q[:], T.q[:])], [], ["Q"], inc=16)
-    op("y", [lambda: g.sync.dma_start(T.RF[:], T.refl[:])], [], ["RF"], inc=16)
 
-    op("g", [lambda: g.iota(T.SELI[0:8, :], [[1, 8], [0, 16]], 0, -1, allow_small_or_imprecise_dtypes=True)], [], ["SELI"])
-    op("g", [lambda: g.iota(T.D[:], [[1, 128]], 0, -1, allow_small_or_imprecise_dtypes=True)], [], ["D"])
+    iota(T.SELI[0:8, :], "SELI", [[1, 8], [0, 16]], -1)
+    op("g", [lambda: g.iota(T.PC[:, 0:1], [[0, 1]], 0, 1)], [], ["PC"])
+    iota(T.I16[:], "I16", [[0, 4], [1, 16]], 0)
+    iota(T.D[:], "D", [[1, 128]], -1)
     op("v", [lambda: V.memset(T.Wb[:], 0.0)], [], ["WbV", "WbS"])
-    op("v", [lambda: V.memset(T.SM[:], 0.0)], [], ["SM"])
-    op("v", [lambda: V.tensor_scalar(T.SEL[0:8, :], T.SELI[0:8, :], 0.0, None, A.is_equal)], ["SELI"], ["SEL"])
-    op("v", [lambda: V.tensor_scalar(T.ID[:], T.D[:], 0.0, None, A.is_equal)], ["D"], ["ID"])
-    op("v", [lambda: tt(T.T64[:], T.ID[:, 0:64], T.ID[:, 64:128], A.add)], ["ID"], ["T64"])
-    op("v", [lambda: tt(T.T32[:], T.T64[:, 0:32], T.T64[:, 32:64], A.add)], ["T64"], ["T32"])
-    op("v", [lambda: tt(T.M16[:], T.T32[:, 0:16], T.T32[:, 16:32], A.add)], ["T32"], ["M16"])
+    op("v", [lambda: V.memset(T.GR[:, TAB:TAB + 16], 0.0)], [], ["GRz"])
+    op("v", [lambda: V.memset(T.DG[:], 0.0)], [], ["DG"])
+    op("v", [lambda: ts(T.SEL[0:8, :], T.SELI[0:8, :], 0.0, None, A.is_equal)], ["SELI"], ["SEL"])
+    op("v", [lambda: ts(T.PCI[:, 0:1], T.PC[:, 0:1], 15, None, A.bitwise_and),
+             lambda: ts(T.PCI[:, 1:2], T.PC[:, 0:1], 1, None, A.bitwise_and),
+             lambda: ts(T.PCI[:, 2:3], T.PC[:, 0:1], 1, 1, A.logical_shift_right, A.bitwise_and)], ["PC"], ["PCI"])
     op("v", [lambda: V.tensor_copy(T.PB[0:8, :, :], T.PXY[0:8, :, :])], ["px", "py"], ["PB"])
-    op("p", [lambda: PE.matmul(T.PI0[:, 0, :, :], T.SEL[0:8, :], T.PB[0:8, :, :], True, True)], ["SEL", "PB"], ["PI0"])
-    op("v", [lambda: V.tensor_copy(T.P[:, 5, :, :], T.PI0[:, 0, :, :])], [], ["PI0", "Pown"])
-    for k, slots in enumerate(GROUPS):
-        send(0, k, [T.P[:, 5, :, :] for s in slots], [T.P[:, s, :, :] for s in slots],
-             [cores[(rank - dist[s]) % NR] for s in slots], ["Pown"])
+    op("p", [lambda: PE.matmul(T.PT0[:, 0:64], T.SEL[0:8, :], T.PB[0:8, :, :], True, True)], ["SEL", "PB"], ["PT0"])
+    op("v", [lambda: V.tensor_copy(T.PCF[:, 0:3], T.PCI[:, 0:3])], ["PCI"], ["PCF"])
+    op("v", [lambda: V.tensor_copy(T.P[:, OWN_SLOT, :, :], T.PT0[:, 0:64])], [], ["PT0", "Pown"])
+    send(0, (0, 1), ["Pown"])
+    if cut < TAB:
+        g.sem_inc(T.sem["go"], 1)
+        g.sync.wait_ge(T.sem["go"], 1)
+        op("y", [lambda: g.sync.dma_start(T.GR[:, cut:TAB], T.green[:, cut:TAB])], [], ["GR1"], inc=16)
+    op("y", [lambda: g.sync.dma_start(T.RF[:], T.refl[:])], [], ["RF"], inc=16)
+    send(0, (2, 3), [])
+    send(0, (4,), [])
+    iota(T.I2[:], "I2", [[0, 16], [1, 2], [0, 3]], 0)
+    iota(T.I4[:], "I4", [[0, 8], [1, 4], [0, 3]], 0)
 
-    op("v", [lambda c=c: V.tensor_scalar(T.MK[:, 16 * c:16 * c + 16], T.M16[:], -128.0 if c < 2 else -1.0, None, A.mult)
-             for c in range(4)], ["M16"], ["MK"])
-    op("v", [lambda: tt(T.TMP[:], T.P[:, 5, :, :], T.MK[:], A.mult)], ["Pown", "MK"], ["TMP"])
+    op("v", [lambda a=a: ts(T.MK[:, 32 * a:32 * a + 32], T.I16[:, 0:32], T.PCF[:, 0:1], (-128.0, -1.0)[a], A.is_equal, A.mult)
+             for a in range(2)], ["I16", "PCF"], ["MK"])
+    op("v", [lambda: ts(T.ID[:], T.D[:], 0.0, None, A.is_equal)], ["D"], ["ID"])
+    op("v", [lambda: tt(T.TMP[:], T.P[:, OWN_SLOT, :, :], T.MK[:], A.mult)], ["Pown", "MK"], ["TMP"])
+    op("v", [lambda h=h: ts(T.DG[:, h, 16 * h:16 * h + 16], T.I16[:, 0:16], T.PCF[:, 0:1], float(TAB), A.is_equal, A.mult)
+             for h in range(2)], ["I16", "PCF"], ["DG"])
     op("v", [lambda c=c: V.tensor_reduce(T.OWN[:, c:c + 1], T.TMP[:, 16 * c:16 * c + 16], AxisListType.X, A.add)
              for c in range(4)], ["TMP"], ["OWN"])
 
-    def offsets_s(a, b, src):
+    def offsets_s(a, b):
+        src = ["Pown" if s == OWN_SLOT else "arr0_%d" % s for s in range(a, b)]
         op("s", [lambda c=c: S.activation(T.AB[:, c, a:b, :], T.P[:, a:b, c // 2, :], ACT.Abs, bias=T.OWN[:, c:c + 1],
-                                          scale=128.0 if c < 2 else 1.0) for c in range(4)], ["OWN", src], ["AB%d" % a])
+                                          scale=128.0 if c < 2 else 1.0) for c in range(4)], ["OWN"] + src, ["AB%d" % a])
 
     def offsets_p(a, b, bank):
-        fns = []
+        fns, n, own = [], 64 * (b - a), a == OWN_SLOT
         for h in range(2):
-            fns.append(lambda h=h: PE.matmul(T[bank][:, h, 0:b - a, :], T.ID[:], T.AB[:, h, a:b, :], True, False))
-            fns.append(lambda h=h: PE.matmul(T[bank][:, h, 0:b - a, :], T.ID[:], T.AB[:, 2 + h, a:b, :], False, True))
-        op("p", fns, ["ID", "AB%d" % a], [bank])
+            fns.append(lambda h=h: PE.matmul(T[bank][:, h:n:2], T.ID[:], T.AB[:, h, a:b, :], True, False))
+            if own:
+                fns.append(lambda h=h: PE.matmul(T[bank][:, h:n:2], T.ID[:], T.DG[:, h, :], False, False))
+            fns.append(lambda h=h: PE.matmul(T[bank][:, h:n:2], T.ID[:], T.AB[:, 2 + h, a:b, :], False, True))
+        op("p", fns, ["ID", "DG", "AB%d" % a], [bank])
 
     def offsets_v(a, b, bank):
-        op("v", [lambda h=h: V.tensor_copy(T.OFF[:, 64 * a + h:64 * b:2], T[bank][:, h, 0:b - a, :]) for h in range(2)],
+        op("v", [lambda: V.tensor_copy(T.OFF[:, 64 * a:64 * b], T[bank][:, 0:64 * (b - a)])],
            [], [bank] + ["OFF%d" % s for s in range(a, b)])
 
-    def gather(q, n):
-        src = lambda: T.GR[:, 0:TAB].indirect(T.OFF[:, 32 * n:32 * n + 32])
-        out = T.G[:, 512 * n:512 * n + 512]
+    def gather(q, a, b):
+        src = lambda: T.GR[:, 0:TAB + 16].indirect(T.OFF[:, 16 * a:16 * b])
+        out = T.G[:, 256 * a:256 * b]
         fn = (lambda: V.tensor_copy(out, src())) if q == "v" else (lambda: S.activation(out, src(), ACT.Copy))
-        op(q, [fn], ["GR", "OFF%d" % (n // 2)], ["G%d" % n])
+        op(q, [fn], ["GR0", "GR1", "GRz"] + ["OFF%d" % s for s in range(a // 4, (b + 3) // 4)], ["G%d" % x for x in range(a, b)])
 
-    def turn(n, m=1):
-        op("v", [lambda: V.transpose(T.Mt[:, 512 * n:512 * (n + m)], T.G[:, 512 * n:512 * (n + m)])],
-           ["G%d" % x for x in range(n, n + m)], ["Mt%d" % x for x in range(n, n + m)])
+    def turn(a, b):
+        op("v", [lambda: V.transpose(T.Mt[:, 256 * a:256 * b], T.G[:, 256 * a:256 * b])],
+           ["G%d" % x for x in range(a, b)], ["Mt%d" % x for x in range(a, b)])
 
     def lay(dst, dkey, mid, mkey, src, skey):
         op("v", [lambda: V.transpose(mid[:], src[:])], [skey], [mkey])
-        op("v", [lambda ab=ab: V.tensor_copy(dst[:, ab:32:2], mid[:, 16 * ab:16 * ab + 16]) for ab in range(2)], [mkey], [dkey])
+        return lambda: op("v", [lambda ab=ab, h=h: V.tensor_copy(dst[:, 2 * h + ab:32:4], mid[:, 16 * ab + 8 * h:16 * ab + 8 * h + 8])
+                                for ab in range(2) for h in range(2)], [mkey], [dkey])
 
     def split_tail():
-        hi, mid, lo = T.Wp[:, 0:96:3], T.Wp[:, 1:96:3], T.Wp[:, 2:96:3]
+        hi, mid = T.Wp[:, :, 0], T.Wp[:, :, 1]
         op("v", [lambda: tt(T.R[:], T.W[:], hi, A.subtract), lambda: tt(mid, T.W[:], hi, A.subtract)],
            ["W", "hi"], ["R", "mid"], "sp1")
-        op("v", [lambda: tt(lo, T.R[:], mid, A.subtract)], ["R", "mid"], ["lo"], "sp2")
-        op("s", [lambda b=b: S.activation(T.Wb[32 * b:32 * b + 32, b, :], T.Wp[32 * b:32 * b + 32, :], ACT.Copy)
-                 for b in (2, 3)], ["hi", "mid", "lo"], ["WbS"], "plS")
-        op("v", [lambda b=b: V.tensor_copy(T.Wb[32 * b:32 * b + 32, b, :], T.Wp[32 * b:32 * b + 32, :])
-                 for b in (0, 1)], ["hi", "mid", "lo"], ["WbV"], "plV")
+        blk = lambda b: slice(32 * b, 32 * b + 32)
+        op("s", [lambda b=b: S.activation(T.Wb[blk(b), b, :, 0:2], T.Wp[blk(b), :, :], ACT.Copy) for b in range(4)],
+           ["hi", "mid"], ["WbS"], "plS")
+        op("v", [lambda b=b: tt(T.Wb[blk(b), b, :, 2], T.R[blk(b), :], T.Wp[blk(b), :, 1], A.subtract) for b in range(4)],
+           ["R", "mid"], ["WbV"], "plV")
 
-    def mm(k, bank=None, c0=0, c1=16):
-        bank = k if bank is None else bank
-        op("p", [lambda c=c: PE.matmul(T["PR%d" % bank][:, :, 6 * c:6 * c + 6], T.Mt[:, 2048 * k + c:2048 * k + 2048:16],
-                                       T.Wb[:, :, 6 * c:6 * c + 6], True, True) for c in range(c0, c1)],
-           ["WbS", "WbV"] + ["Mt%d" % x for x in range(4 * k, 4 * k + 4)], ["PR%d" % bank], "mm%d" % bank)
+    def mm(o, reg, c0=0, c1=96, bank=None):
+        slots, e, bank = reg[0], reg[1], bank or reg[2]
+        x0, x1 = 1024 * slots[0], 1024 * slots[-1] + 1024
+        if len(slots) == 1:
+            fns = [lambda c=c: PE.matmul(T[bank][:, :, 12 * c:12 * c + 12], T.Mt[:, x0 + c:x1:8],
+                                         T.Wb[:, :, 4 * c:4 * c + 4, :], True, True) for c in range(c0 // 12, c1 // 12)]
+        else:
+            at = (lambda c: 6 * c) if o == ORD - 1 else (lambda c: 12 * (c % 8) + 6 * (c // 8))
+            fns = [lambda c=c, x=4 * (c % 8) + 2 * (c // 8): PE.matmul(T[bank][:, :, at(c):at(c) + 6], T.Mt[:, x0 + c:x1:16],
+                                                                       T.Wb[:, :, x:x + 2, :], True, True)
+                   for c in range(16) if c0 <= at(c) < c1]
+        op("p", fns, ["WbS", "WbV"] + ["Mt%d" % x for x in range(x0 // 256, x1 // 256)],
+           [bank + "_%d" % b for b in range(4)], "mm" + bank)
 
-    def scan(k, bank=None, c0=0, c1=16):
-        bank = k if bank is None else bank
-        keys = ["E%d_%d" % (k, h) for h in range(c0 // 8, c1 // 8)]
-        op("v", [lambda b=b: V.tensor_tensor_scan(T["E%d" % k][:, b, 6 * c0:6 * c1], T["PR%d" % bank][:, b, 6 * c0:6 * c1],
-                                                  T.SM[:, 6 * c0:6 * c1], 0.0, A.add, A.mult) for b in range(4)],
-           ["SM"], ["PR%d" % bank] + keys, "scan%d" % bank)
+    def scan(reg, b0=0, b1=4, c0=0, c1=96, bank=None):
+        slots, e, bank = reg[0], reg[1], bank or reg[2]
+        mask = "SM%d" % (4 // len(slots))
+        op("v", [lambda b=b: V.tensor_tensor_scan(T[e][:, b, c0:c1], T[bank][:, b, c0:c1], T[mask][:, c0:c1], 0.0, A.add, A.mult)
+                 for b in range(b0, b1)], [mask],
+           ["%s_%d" % (bank, b) for b in range(b0, b1)] + ["%s_%d_%d" % (e, b, c0 > 0) for b in range(b0, b1)],
+           "scan%s_%d" % (bank, b0))
 
-    def back(k):
-        op("p", [lambda: PE.matmul(T["PT%d" % k][:, 0, :, :], T["E%d" % k][:, :, 2:96:3], T.S2[:], True, True)],
-           ["E%d_0" % k, "E%d_1" % k, "S2"], ["PT%d" % k], "back%d" % k)
+    def back(reg):
+        slots, e, _, bank = reg
+        sel = "S%d" % (4 // len(slots))
+        op("p", [lambda: PE.matmul(T[bank][:, 0:32 * len(slots)], T[e][:, :, 2:96:3], T[sel][:], True, True)],
+           ["%s_%d_%d" % (e, b, h) for b in range(4) for h in range(2)] + [sel], [bank], "back" + bank)
 
-    def out(o, k):
-        key = "Sb%d_%d" % (o, k)
-        op("v", [lambda: V.transpose(T.Sb[:, o, 64 * k:64 * k + 64], T["PT%d" % k][:, 0, :, :])], [], ["PT%d" % k, key], "out%d" % k)
-        slots = GROUPS[k]
-        send(o + 1, k, [T.Sb[:, o, 32 * s:32 * s + 32] for s in slots], [T.L[:, o, 32 * s:32 * s + 32] for s in slots],
-             [cores[(rank + dist[s]) % NR] for s in slots], [key])
+    def out(o, reg):
+        slots, e, _, bank = reg
+        dst, src = T.Sb[:, o, 32 * slots[0]:32 * slots[-1] + 32], T[bank][:, 0:32 * len(slots)]
+        keys = [bank] + ["Sb%d_%d" % (o, s) for s in slots]
+        op("v", [lambda: V.transpose(dst, src)], [], keys, "out" + bank)
+        far = tuple(s for s in slots if s != OWN_SLOT)
+        if far:
+            send(o + 1, far, keys[1:])
 
-    def receive(o):
-        land = lambda s: T.L[:, o, 32 * s:32 * s + 32]
-        own, ownkey = T.Sb[:, o, 160:192], "Sb%d_2" % o
+    part = lambda o, s: (T.Sb[:, o, 32 * s:32 * s + 32], "Sb%d_%d" % (o, s)) if s == OWN_SLOT else (
+        T.L[:, o, 32 * s:32 * s + 32], "arr%d_%d" % (o + 1, s))
+
+    def add(n, a, b):
+        op("v", [lambda: tt(T.AC[:, n, :], a[0], b[0], A.add)], [a[1], b[1]], ["AC%d" % n], "add%d" % n)
+        return T.AC[:, n, :], "AC%d" % n
+
+    def finish(o, acc, s):
+        last, fkey = part(o, s), "F%d" % o
         if o == ORD - 1:
-            op("v", [lambda: tt(T.A0[:], own, T.YB[:], A.add)], [ownkey, "YB"], ["A0"])
-            own, ownkey = T.A0[:], "A0"
-        op("v", [lambda: tt(T.U[:], land(0), land(1), A.add)], ["arr%d_0" % (o + 1)], ["U"], "u")
-        op("v", [lambda: tt(T.A1[:], T.U[:], own, A.add)], ["U", ownkey], ["A1"], "a1")
-        op("v", [lambda: tt(T.Z[:], land(2), land(3), A.add)], ["arr%d_1" % (o + 1)], ["Z"], "z")
-        op("v", [lambda: tt(T.A2[:], T.A1[:], T.Z[:], A.add)], ["A1", "Z"], ["A2"], "a2")
-        if o == ORD - 1:
-            op("v", [lambda ab=ab: tt(T.F[:, o, 16 * ab:16 * ab + 16], T.A2[:, ab:32:2], T.L[:, o, 128 + ab:160:2], A.add)
-                     for ab in range(2)], ["A2", "arr%d_2" % (o + 1)], ["F%d" % o])
-            op("v", [lambda: V.transpose(T.YN[:], T.F[:, o, :])], ["F%d" % o], ["YN"])
+            n = int(acc[1][2:])
+            op("v", [lambda ab=ab: tt(T.F[:, o, 16 * ab:16 * ab + 16], T.AC[:, n, ab:32:2], T.L[:, o, 32 * s + ab:32 * s + 32:2], A.add)
+                     for ab in range(2)], [acc[1], last[1]], [fkey])
+            op("v", [lambda: V.transpose(T.YN[:], T.F[:, o, :])], [fkey], ["YN"])
             op("y", [lambda: g.sync.dma_start(T.y[:], T.YN[:])], ["YN"], ["y"], inc=16)
             return
-        op("v", [lambda: tt(T.F[:, o, :], T.A2[:], land(4), A.add)], ["A2", "arr%d_2" % (o + 1)], ["F%d" % o], "f")
-        op("v", [lambda: tt(T.Wp[:, 0:96:3], T.F[:, o, :], T.RT[:], A.mult), lambda: tt(T.W[:], T.F[:, o, :], T.RT[:], A.mult)],
-           ["F%d" % o, "RT"], ["W", "hi"], "sp0")
+        op("v", [lambda: tt(T.F[:, o, :], acc[0], last[0], A.add)], [acc[1], last[1]], [fkey], "addf")
+        op("v", [lambda: tt(T.Wp[:, :, 0], T.F[:, o, :], T.RT[:], A.mult), lambda: tt(T.W[:], T.F[:, o, :], T.RT[:], A.mult)],
+           [fkey, "RT"], ["W", "hi"], "sp0")
         split_tail()
-        if o == 1:
-            op("v", [lambda: tt(T.YA[:], T.F[:, 0, :], T.F[:, 1, :], A.add)], ["F0", "F1"], ["YA"])
-        if o == 2:
-            op("v", [lambda: tt(T.YB[:], T.YA[:], T.F[:, 2, :], A.add)], ["YA", "F2"], ["YB"])
 
-    offsets_s(5, 6, "Pown")
-    offsets_p(5, 6, "PT2")
+    offsets_s(5, 6)
+    q2 = lay(T.W, "W", T.QT, "QT", T.Q, "Q")
     op("v", [lambda: tt(T.S2[:], T.ID[:, 0:128:2], T.ID[:, 1:128:2], A.add)], ["ID"], ["S2"])
-    op("v", [lambda: V.tensor_reduce(T.PAR[:, 0:1], T.M16[:, 0:16:2], AxisListType.X, A.add),
-             lambda: V.tensor_reduce(T.PAR[:, 1:2], T.M16[:, 1:16:2], AxisListType.X, A.add)], ["M16"], ["PAR"])
-    offsets_v(5, 6, "PT2")
-    op("v", [lambda c=c: V.tensor_scalar(T.SM[:, c:96:6], T.SM[:, c:96:6], T.PAR[:, c // 3:c // 3 + 1], None, A.add)
-             for c in range(6)], ["PAR"], ["SM"])
-    lay(T.W, "W", T.QT, "QT", T.Q, "Q")
-    op("v", [lambda: V.tensor_copy(T.Wp[:, 0:96:3], T.W[:])], ["W"], ["hi"])
+    q2()
+    op("v", [lambda: ts(T.PCF[:, 3:4], T.PCF[:, 1:2], 2.0, T.PCF[:, 2:3], A.mult, A.add)], ["PCF"], ["PC4"])
+    offsets_p(5, 6, "PT3")
+    op("v", [lambda: V.tensor_copy(T.Wp[:, :, 0], T.W[:])], ["W"], ["hi"])
+    op("v", [lambda: tt(T.S4[:], T.S2[:, 0:64:2], T.S2[:, 1:64:2], A.add)], ["S2"], ["S4"])
+    offsets_v(5, 6, "PT3")
     split_tail()
+    op("v", [lambda: ts(T.SM2[:], T.I2[:], T.PCF[:, 1:2], None, A.is_equal)], ["I2", "PCF"], ["SM2"])
+    op("v", [lambda: ts(T.SM4[:], T.I4[:], T.PCF[:, 3:4], None, A.is_equal)], ["I4", "PC4"], ["SM4"])
 
-    gather("s", 10)
-    gather("v", 11)
-    op("v", [lambda: V.memset(T.G[:, 5120:6144:33], 0.0)], [], ["G10", "G11"])
-    turn(10, 2)
-    offsets_s(0, 2, "arr0_0")
-    offsets_p(0, 2, "PI0")
-    offsets_v(0, 2, "PI0")
-    gather("s", 0)
-    gather("v", 3)
-    offsets_s(2, 4, "arr0_1")
-    offsets_p(2, 4, "PT2")
-    gather("s", 1)
-    offsets_s(4, 5, "arr0_2")
-    offsets_p(4, 5, "PI0")
-    turn(3)
-    turn(0)
-    offsets_v(2, 4, "PT2")
-    gather("v", 7)
-    gather("s", 2)
-    gather("s", 4)
-    turn(1)
-    offsets_v(4, 5, "PI0")
-    turn(7)
-    turn(2)
-    mm(0)
-    gather("s", 5)
-    gather("s", 6)
-    gather("s", 8)
-    gather("v", 9)
-    scan(0)
-    back(0)
-    turn(4)
-    out(0, 0)
-    turn(5)
-    turn(9)
-    turn(6)
-    mm(1)
-    scan(1)
-    back(1)
-    turn(8)
-    mm(2)
-    out(0, 1)
-    scan(2)
-    back(2)
-    out(0, 2)
-    lay(T.RT, "RT", T.RN, "RN", T.RF, "RF")
-    receive(0)
+    def run(o, layout, steps):
+        regs = [(s, "E%d" % k, "PR%d" % k, "PT%d" % k) for k, s in enumerate(layout)]
+        sums, later = {}, []
+        val = lambda x: sums[x] if x in sums else part(o, int(x))
+        for st in steps.split():
+            w, a = st[0], st[1:].split(",")
+            if w in "SV":
+                gather(w.lower(), int(a[0]), int(a[1]))
+            elif w == "t":
+                turn(int(a[0]), int(a[1]))
+            elif w == "A":
+                offsets_s(int(a[0]), int(a[1]))
+                offsets_p(int(a[0]), int(a[1]), "PT" + a[2])
+            elif w == "C":
+                offsets_v(int(a[0]), int(a[1]), "PT" + a[2])
+            elif w in "ms":
+                reg, kw = regs[int(a[0][0])], {}
+                if a[0][1:] == "a":
+                    kw = {"c0": 0, "c1": 48}
+                if a[0][1:] == "b":
+                    kw = {"c0": 48, "c1": 96, "bank": "PR3"}
+                if w == "m":
+                    mm(o, reg, **kw)
+                else:
+                    scan(reg, *[int(x) for x in a[1:]], **kw)
+            elif w == "b":
+                back(regs[int(a[0])])
+            elif w == "o":
+                out(o, regs[int(a[0])])
+            elif w == "+":
+                sums[a[0]] = add(len(sums), val(a[1]), val(a[2]))
+            elif w == "r":
+                if a[0] == "1":
+                    later.append(lay(T.RT, "RT", T.RN, "RN", T.RF, "RF"))
+                else:
+                    later.pop()()
+            elif w == "y":
+                if a[0] == "1" and o == 2:
+                    op("v", [lambda: tt(T.YA[:], T.F[:, 0, :], T.F[:, 1, :], A.add)], ["F0", "F1"], ["YA"])
+                if a[0] == "1" and o == 3:
+                    op("v", [lambda: tt(T.YB[:], T.YA[:], T.F[:, 2, :], A.add)], ["YA", "F2"], ["YB"])
+                if a[0] == "2":
+                    op("v", [lambda ab=ab, h=h: V.tensor_copy(T.AR[:, 16 * h + ab:16 * h + 16:2], T.YB[:, 2 * h + ab:32:4])
+                             for ab in range(2) for h in range(2)], ["YB"], ["AR"])
+                    sums["Y"] = (T.AR[:], "AR")
+            elif w == "f":
+                finish(o, val(a[0]), int(a[1]))
 
-    for o in range(1, ORD):
-        mm(0, 0, 0, 8)
-        mm(0, 3, 8, 16)
-        mm(1)
-        scan(0, 0, 0, 8)
-        scan(0, 3, 8, 16)
-        back(0)
-        mm(2)
-        out(o, 0)
-        scan(1)
-        back(1)
-        scan(2)
-        back(2)
-        out(o, 1)
-        out(o, 2)
-        receive(o)
+    run(0, *CFG["o1"])
+    run(1, *CFG["mid"])
+    run(2, *CFG["mid"])
+    run(3, *CFG["last"])
 
     for name, n in cnt.items():
         if waited.get(name, 0) < n:

from concourse.bass import DstId, RemoteDMATransfer
from concourse.mybir import AluOpType, AxisListType, ActivationFunctionType

NR, NS, ORD, TAB = 6, 32, 4, 6144
OWN_SLOT = NR - 1
NLOC = 120
L3, L4 = ((0, 1), (2, 3), (4, 5)), ((0, 1), (2, 3), (4,), (5,))
CFG = {
    "split": 0,
    "o1": (L4, "A0,2,0 S20,21 V21,22 C0,2,0 A2,5,1 V6,8 S0,2 C2,5,1 t6,8 S2,4 t0,2 V14,16 S4,6 t2,4 t14,16 S8,10 t4,6 m0 "
               "V18,20 S10,12 s0 b0 t8,10 o0 S12,14 t18,20 t10,12 S16,17 t20,22 S17,18 t12,14 m1 t16,17 S22,24 t17,18 m2 "
               "s1 b1 s2 b2 o1 t22,24 m3 o2 r1 s3 b3 r2 o3 +u,0,1 +z,2,3 +w,u,5 +x,w,z fx,4"),
    "mid": (L3, "m0 m1 m2a s0 b0 m2b s1 b1 o0 s2a o1 s2b b2 y1 o2 +u,0,1 +w,u,5 +z,2,3 +x,w,z fx,4"),
    "last": (L3, "m0 m1 m2a s0 b0 m2b s1 b1 o0 s2a o1 s2b b2 y1 o2 y2 +u,0,1 +v,u,Y +w,v,5 +z,2,3 +x,w,z fx,4"),
}

SCRATCH = {
    "PXY": ("sbuf", [128, 2, 32], "int32"),
    "PB": ("sbuf", [128, 2, 32], "bfloat16"),
    "P": ("sbuf", [128, 6, 2, 32], "bfloat16"),
    "GR": ("sbuf", [128, TAB + 16], "bfloat16"),
    "G": ("sbuf", [128, 6144], "bfloat16"),
    "Mt": ("sbuf", [128, 6144], "bfloat16"),
    "OFF": ("sbuf", [128, 384], "uint16"),
    "AB": ("sbuf", [128, 4, 6, 32], "bfloat16"),
    "DG": ("sbuf", [128, 2, 32], "bfloat16"),
    "SELI": ("sbuf", [128, 128], "float32"),
    "SEL": ("sbuf", [128, 128], "bfloat16"),
    "D": ("sbuf", [128, 128], "float32"),
    "ID": ("sbuf", [128, 128], "bfloat16"),
    "S2": ("sbuf", [128, 64], "float32"),
    "S4": ("sbuf", [128, 32], "float32"),
    "IM": ("sbuf", [128, 8, 16], "float32"),
    "M16": ("sbuf", [128, 16], "float32"),
    "MK": ("sbuf", [128, 64], "float32"),
    "TMP": ("sbuf", [128, 64], "float32"),
    "OWN": ("sbuf", [128, 4], "float32"),
    "PC": ("sbuf", [128, 8], "int32"),
    "PCI": ("sbuf", [128, 8], "int32"),
    "PCF": ("sbuf", [128, 8], "float32"),
    "I16": ("sbuf", [128, 64], "float32"),
    "I2": ("sbuf", [128, 96], "float32"),
    "I4": ("sbuf", [128, 96], "float32"),
    "SM2": ("sbuf", [128, 96], "float32"),
    "SM4": ("sbuf", [128, 96], "float32"),
    "Wb": ("sbuf", [128, 4, 32, 3], "bfloat16"),
    "Wp": ("sbuf", [128, 32, 2], "bfloat16"),
    "E0": ("sbuf", [128, 4, 96], "float32"),
    "E1": ("sbuf", [128, 4, 96], "float32"),
    "E2": ("sbuf", [128, 4, 96], "float32"),
    "E3": ("sbuf", [128, 4, 96], "float32"),
    "AR": ("sbuf", [128, 32], "float32"),
    "Sb": ("sbuf", [128, ORD, 192], "float32"),
    "L": ("sbuf", [128, ORD, 160], "float32"),
    "Q": ("sbuf", [128, 32], "float32"),
    "QT": ("sbuf", [128, 32], "float32"),
    "RF": ("sbuf", [128, 32], "float32"),
    "RN": ("sbuf", [128, 32], "float32"),
    "RT": ("sbuf", [128, 32], "float32"),
    "W": ("sbuf", [128, 32], "float32"),
    "R": ("sbuf", [128, 32], "float32"),
    "AC": ("sbuf", [128, 6, 32], "float32"),
    "F": ("sbuf", [128, ORD, 32], "float32"),
    "YA": ("sbuf", [128, 32], "float32"),
    "YB": ("sbuf", [128, 32], "float32"),
    "YN": ("sbuf", [128, 32], "float32"),
    "PR0": ("psum", [128, 4, 128], "float32"),
    "PR1": ("psum", [128, 4, 128], "float32"),
    "PR2": ("psum", [128, 4, 128], "float32"),
    "PR3": ("psum", [128, 4, 128], "float32"),
    "PT0": ("psum", [128, 512], "float32"),
    "PT1": ("psum", [128, 512], "float32"),
    "PT2": ("psum", [128, 512], "float32"),
    "PT3": ("psum", [128, 512], "float32"),
}
SEMAPHORES = (["sent", "go"] + ["arr%d_%d" % (o, k) for o in range(ORD + 1) for k in range(NR - 1)]
              + ["s%d" % k for k in range(NLOC)])


def rank_program(g, core, T, topo):
    rank = T.rank_of(core)
    if rank is None:
        return
    cores = list(T.cores)
    A, ACT = AluOpType, ActivationFunctionType
    V, S, PE = g.vector, g.scalar, g.tensor
    queue = {"g": g, "v": V, "s": S, "p": PE, "y": g.sync}

    def hops(a, b):
        ca, cb = topo.chip(a), topo.chip(b)
        return 0 if ca == cb else (1 if topo.mates(ca, cb) or topo.same_plane(ca, cb) else 2)
    dist = sorted(range(1, NR), key=lambda d: (-sum(hops(cores[r], cores[(r + d) % NR]) for r in range(NR)), d))

    cnt, waited, site, res = {}, {}, {}, {}
    know = {q: {} for q in queue}

    def need(q, ev):
        name, n, kn = ev
        if know[q].get(name, 0) >= n:
            return
        queue[q].wait_ge(T.sem[name], n)
        waited[name] = max(waited.get(name, 0), n)
        know[q][name] = n
        for k, v in kn.items():
            if know[q].get(k, 0) < v:
                know[q][k] = v

    def before(q, reads, writes):
        evs = []
        for r in reads:
            evs += res.setdefault(r, [[], []])[0]
        for w in writes:
            e = res.setdefault(w, [[], []])
            evs += e[0] + e[1]
        for ev in reversed(evs):
            need(q, ev)

    def op(q, fns, reads, writes, name=None, inc=1):
        before(q, reads, writes)
        if name is None:
            name = "once%d" % len(site)
        if name not in site:
            site[name] = "s%d" % len(site)
        sem = site[name]
        for fn in fns:
            fn().then_inc(T.sem[sem], inc)
            cnt[sem] = cnt.get(sem, 0) + inc
        ev = (sem, cnt[sem], dict(know[q]))
        for r in reads:
            res[r][1].append(ev)
        for w in writes:
            res[w] = [[ev], []]

    def send(rnd, slots, reads):
        before("g", reads, [])
        trs = []
        for n, s in enumerate(slots):
            name = "arr%d_%d" % (rnd, s)
            ahead, behind = cores[(rank + dist[s]) % NR], cores[(rank - dist[s]) % NR]
            if rnd == 0:
                peer, sender, src, dst = behind, ahead, T.P[:, OWN_SLOT, :, :], T.P[:, s, :, :]
            else:
                peer, sender = ahead, behind
                src, dst = T.Sb[:, rnd - 1, 32 * s:32 * s + 32], T.L[:, rnd - 1, 32 * s:32 * s + 32]
            eng = topo.engines(core, peer)
            share = len(eng) // len(slots)
            m = sum(1 << e for e in eng[n * share:(n + 1) * share])
            rid, pid = topo.addr(peer)[0:2]
            cnt["sent"] = cnt.get("sent", 0) + share
            cnt[name] = len(topo.engines(sender, core)) // len(slots)
            res[name] = [[(name, cnt[name], {})], []]
            if len(slots) == 1:
                g.remote_dma(dst, src, T.sem[name], T.sem["sent"], pid, rid, m)
            else:
                trs.append(RemoteDMATransfer(dst_ids=[DstId(rid=rid, pnc=pid)], dma_engine_mask=m, remote_sem=T.sem[name],
                                             src=src, dst=dst))
        if trs:
            g.remote_dma_fused(trs, local_sem=T.sem["sent"])

    tt, ts = V.tensor_tensor, V.tensor_scalar

    def iota(out, key, pattern, mult):
        op("g", [lambda: g.iota(out, pattern, 0, mult, allow_small_or_imprecise_dtypes=True)], [], [key])

    cut = CFG["split"] or TAB
    op("y", [lambda: g.sync.dma_start(T.PXY[0:8, 0, :], T.px[:])], [], ["px"], inc=16)
    op("s", [lambda: S.dma_start(T.PXY[0:8, 1, :], T.py[:])], [], ["py"], inc=16)
    op("y", [lambda: g.sync.dma_start(T.GR[:, 0:cut], T.green[:, 0:cut])], [], ["GR0"], inc=16)
    op("s", [lambda: S.dma_start(T.Q[:], T.q[:])], [], ["Q"], inc=16)

    iota(T.SELI[0:8, :], "SELI", [[1, 8], [0, 16]], -1)
    op("g", [lambda: g.iota(T.PC[:, 0:1], [[0, 1]], 0, 1)], [], ["PC"])
    iota(T.I16[:], "I16", [[0, 4], [1, 16]], 0)
    iota(T.D[:], "D", [[1, 128]], -1)
    op("v", [lambda: V.memset(T.Wb[:], 0.0)], [], ["WbV", "WbS"])
    op("v", [lambda: V.memset(T.GR[:, TAB:TAB + 16], 0.0)], [], ["GRz"])
    op("v", [lambda: V.memset(T.DG[:], 0.0)], [], ["DG"])
    op("v", [lambda: ts(T.SEL[0:8, :], T.SELI[0:8, :], 0.0, None, A.is_equal)], ["SELI"], ["SEL"])
    op("v", [lambda: ts(T.PCI[:, 0:1], T.PC[:, 0:1], 15, None, A.bitwise_and),
             lambda: ts(T.PCI[:, 1:2], T.PC[:, 0:1], 1, None, A.bitwise_and),
             lambda: ts(T.PCI[:, 2:3], T.PC[:, 0:1], 1, 1, A.logical_shift_right, A.bitwise_and)], ["PC"], ["PCI"])
    op("v", [lambda: V.tensor_copy(T.PB[0:8, :, :], T.PXY[0:8, :, :])], ["px", "py"], ["PB"])
    op("p", [lambda: PE.matmul(T.PT0[:, 0:64], T.SEL[0:8, :], T.PB[0:8, :, :], True, True)], ["SEL", "PB"], ["PT0"])
    op("v", [lambda: V.tensor_copy(T.PCF[:, 0:3], T.PCI[:, 0:3])], ["PCI"], ["PCF"])
    op("v", [lambda: V.tensor_copy(T.P[:, OWN_SLOT, :, :], T.PT0[:, 0:64])], [], ["PT0", "Pown"])
    send(0, (0, 1), ["Pown"])
    if cut < TAB:
        g.sem_inc(T.sem["go"], 1)
        g.sync.wait_ge(T.sem["go"], 1)
        op("y", [lambda: g.sync.dma_start(T.GR[:, cut:TAB], T.green[:, cut:TAB])], [], ["GR1"], inc=16)
    op("y", [lambda: g.sync.dma_start(T.RF[:], T.refl[:])], [], ["RF"], inc=16)
    send(0, (2, 3), [])
    send(0, (4,), [])
    iota(T.I2[:], "I2", [[0, 16], [1, 2], [0, 3]], 0)
    iota(T.I4[:], "I4", [[0, 8], [1, 4], [0, 3]], 0)

    op("v", [lambda a=a: ts(T.MK[:, 32 * a:32 * a + 32], T.I16[:, 0:32], T.PCF[:, 0:1], (-128.0, -1.0)[a], A.is_equal, A.mult)
             for a in range(2)], ["I16", "PCF"], ["MK"])
    op("v", [lambda: ts(T.ID[:], T.D[:], 0.0, None, A.is_equal)], ["D"], ["ID"])
    op("v", [lambda: tt(T.TMP[:], T.P[:, OWN_SLOT, :, :], T.MK[:], A.mult)], ["Pown", "MK"], ["TMP"])
    op("v", [lambda h=h: ts(T.DG[:, h, 16 * h:16 * h + 16], T.I16[:, 0:16], T.PCF[:, 0:1], float(TAB), A.is_equal, A.mult)
             for h in range(2)], ["I16", "PCF"], ["DG"])
    op("v", [lambda c=c: V.tensor_reduce(T.OWN[:, c:c + 1], T.TMP[:, 16 * c:16 * c + 16], AxisListType.X, A.add)
             for c in range(4)], ["TMP"], ["OWN"])

    def offsets_s(a, b):
        src = ["Pown" if s == OWN_SLOT else "arr0_%d" % s for s in range(a, b)]
        op("s", [lambda c=c: S.activation(T.AB[:, c, a:b, :], T.P[:, a:b, c // 2, :], ACT.Abs, bias=T.OWN[:, c:c + 1],
                                          scale=128.0 if c < 2 else 1.0) for c in range(4)], ["OWN"] + src, ["AB%d" % a])

    def offsets_p(a, b, bank):
        fns, n, own = [], 64 * (b - a), a == OWN_SLOT
        for h in range(2):
            fns.append(lambda h=h: PE.matmul(T[bank][:, h:n:2], T.ID[:], T.AB[:, h, a:b, :], True, False))
            if own:
                fns.append(lambda h=h: PE.matmul(T[bank][:, h:n:2], T.ID[:], T.DG[:, h, :], False, False))
            fns.append(lambda h=h: PE.matmul(T[bank][:, h:n:2], T.ID[:], T.AB[:, 2 + h, a:b, :], False, True))
        op("p", fns, ["ID", "DG", "AB%d" % a], [bank])

    def offsets_v(a, b, bank):
        op("v", [lambda: V.tensor_copy(T.OFF[:, 64 * a:64 * b], T[bank][:, 0:64 * (b - a)])],
           [], [bank] + ["OFF%d" % s for s in range(a, b)])

    def gather(q, a, b):
        src = lambda: T.GR[:, 0:TAB + 16].indirect(T.OFF[:, 16 * a:16 * b])
        out = T.G[:, 256 * a:256 * b]
        fn = (lambda: V.tensor_copy(out, src())) if q == "v" else (lambda: S.activation(out, src(), ACT.Copy))
        op(q, [fn], ["GR0", "GR1", "GRz"] + ["OFF%d" % s for s in range(a // 4, (b + 3) // 4)], ["G%d" % x for x in range(a, b)])

    def turn(a, b):
        op("v", [lambda: V.transpose(T.Mt[:, 256 * a:256 * b], T.G[:, 256 * a:256 * b])],
           ["G%d" % x for x in range(a, b)], ["Mt%d" % x for x in range(a, b)])

    def lay(dst, dkey, mid, mkey, src, skey):
        op("v", [lambda: V.transpose(mid[:], src[:])], [skey], [mkey])
        return lambda: op("v", [lambda ab=ab, h=h: V.tensor_copy(dst[:, 2 * h + ab:32:4], mid[:, 16 * ab + 8 * h:16 * ab + 8 * h + 8])
                                for ab in range(2) for h in range(2)], [mkey], [dkey])

    def split_tail():
        hi, mid = T.Wp[:, :, 0], T.Wp[:, :, 1]
        op("v", [lambda: tt(T.R[:], T.W[:], hi, A.subtract), lambda: tt(mid, T.W[:], hi, A.subtract)],
           ["W", "hi"], ["R", "mid"], "sp1")
        blk = lambda b: slice(32 * b, 32 * b + 32)
        op("s", [lambda b=b: S.activation(T.Wb[blk(b), b, :, 0:2], T.Wp[blk(b), :, :], ACT.Copy) for b in range(4)],
           ["hi", "mid"], ["WbS"], "plS")
        op("v", [lambda b=b: tt(T.Wb[blk(b), b, :, 2], T.R[blk(b), :], T.Wp[blk(b), :, 1], A.subtract) for b in range(4)],
           ["R", "mid"], ["WbV"], "plV")

    def mm(o, reg, c0=0, c1=96, bank=None):
        slots, e, bank = reg[0], reg[1], bank or reg[2]
        x0, x1 = 1024 * slots[0], 1024 * slots[-1] + 1024
        if len(slots) == 1:
            fns = [lambda c=c: PE.matmul(T[bank][:, :, 12 * c:12 * c + 12], T.Mt[:, x0 + c:x1:8],
                                         T.Wb[:, :, 4 * c:4 * c + 4, :], True, True) for c in range(c0 // 12, c1 // 12)]
        else:
            at = (lambda c: 6 * c) if o == ORD - 1 else (lambda c: 12 * (c % 8) + 6 * (c // 8))
            fns = [lambda c=c, x=4 * (c % 8) + 2 * (c // 8): PE.matmul(T[bank][:, :, at(c):at(c) + 6], T.Mt[:, x0 + c:x1:16],
                                                                       T.Wb[:, :, x:x + 2, :], True, True)
                   for c in range(16) if c0 <= at(c) < c1]
        op("p", fns, ["WbS", "WbV"] + ["Mt%d" % x for x in range(x0 // 256, x1 // 256)],
           [bank + "_%d" % b for b in range(4)], "mm" + bank)

    def scan(reg, b0=0, b1=4, c0=0, c1=96, bank=None):
        slots, e, bank = reg[0], reg[1], bank or reg[2]
        mask = "SM%d" % (4 // len(slots))
        op("v", [lambda b=b: V.tensor_tensor_scan(T[e][:, b, c0:c1], T[bank][:, b, c0:c1], T[mask][:, c0:c1], 0.0, A.add, A.mult)
                 for b in range(b0, b1)], [mask],
           ["%s_%d" % (bank, b) for b in range(b0, b1)] + ["%s_%d_%d" % (e, b, c0 > 0) for b in range(b0, b1)],
           "scan%s_%d" % (bank, b0))

    def back(reg):
        slots, e, _, bank = reg
        sel = "S%d" % (4 // len(slots))
        op("p", [lambda: PE.matmul(T[bank][:, 0:32 * len(slots)], T[e][:, :, 2:96:3], T[sel][:], True, True)],
           ["%s_%d_%d" % (e, b, h) for b in range(4) for h in range(2)] + [sel], [bank], "back" + bank)

    def out(o, reg):
        slots, e, _, bank = reg
        dst, src = T.Sb[:, o, 32 * slots[0]:32 * slots[-1] + 32], T[bank][:, 0:32 * len(slots)]
        keys = [bank] + ["Sb%d_%d" % (o, s) for s in slots]
        op("v", [lambda: V.transpose(dst, src)], [], keys, "out" + bank)
        far = tuple(s for s in slots if s != OWN_SLOT)
        if far:
            send(o + 1, far, keys[1:])

    part = lambda o, s: (T.Sb[:, o, 32 * s:32 * s + 32], "Sb%d_%d" % (o, s)) if s == OWN_SLOT else (
        T.L[:, o, 32 * s:32 * s + 32], "arr%d_%d" % (o + 1, s))

    def add(n, a, b):
        op("v", [lambda: tt(T.AC[:, n, :], a[0], b[0], A.add)], [a[1], b[1]], ["AC%d" % n], "add%d" % n)
        return T.AC[:, n, :], "AC%d" % n

    def finish(o, acc, s):
        last, fkey = part(o, s), "F%d" % o
        if o == ORD - 1:
            n = int(acc[1][2:])
            op("v", [lambda ab=ab: tt(T.F[:, o, 16 * ab:16 * ab + 16], T.AC[:, n, ab:32:2], T.L[:, o, 32 * s + ab:32 * s + 32:2], A.add)
                     for ab in range(2)], [acc[1], last[1]], [fkey])
            op("v", [lambda: V.transpose(T.YN[:], T.F[:, o, :])], [fkey], ["YN"])
            op("y", [lambda: g.sync.dma_start(T.y[:], T.YN[:])], ["YN"], ["y"], inc=16)
            return
        op("v", [lambda: tt(T.F[:, o, :], acc[0], last[0], A.add)], [acc[1], last[1]], [fkey], "addf")
        op("v", [lambda: tt(T.Wp[:, :, 0], T.F[:, o, :], T.RT[:], A.mult), lambda: tt(T.W[:], T.F[:, o, :], T.RT[:], A.mult)],
           [fkey, "RT"], ["W", "hi"], "sp0")
        split_tail()

    offsets_s(5, 6)
    q2 = lay(T.W, "W", T.QT, "QT", T.Q, "Q")
    op("v", [lambda: tt(T.S2[:], T.ID[:, 0:128:2], T.ID[:, 1:128:2], A.add)], ["ID"], ["S2"])
    q2()
    op("v", [lambda: ts(T.PCF[:, 3:4], T.PCF[:, 1:2], 2.0, T.PCF[:, 2:3], A.mult, A.add)], ["PCF"], ["PC4"])
    offsets_p(5, 6, "PT3")
    op("v", [lambda: V.tensor_copy(T.Wp[:, :, 0], T.W[:])], ["W"], ["hi"])
    op("v", [lambda: tt(T.S4[:], T.S2[:, 0:64:2], T.S2[:, 1:64:2], A.add)], ["S2"], ["S4"])
    offsets_v(5, 6, "PT3")
    split_tail()
    op("v", [lambda: ts(T.SM2[:], T.I2[:], T.PCF[:, 1:2], None, A.is_equal)], ["I2", "PCF"], ["SM2"])
    op("v", [lambda: ts(T.SM4[:], T.I4[:], T.PCF[:, 3:4], None, A.is_equal)], ["I4", "PC4"], ["SM4"])

    def run(o, layout, steps):
        regs = [(s, "E%d" % k, "PR%d" % k, "PT%d" % k) for k, s in enumerate(layout)]
        sums, later = {}, []
        val = lambda x: sums[x] if x in sums else part(o, int(x))
        for st in steps.split():
            w, a = st[0], st[1:].split(",")
            if w in "SV":
                gather(w.lower(), int(a[0]), int(a[1]))
            elif w == "t":
                turn(int(a[0]), int(a[1]))
            elif w == "A":
                offsets_s(int(a[0]), int(a[1]))
                offsets_p(int(a[0]), int(a[1]), "PT" + a[2])
            elif w == "C":
                offsets_v(int(a[0]), int(a[1]), "PT" + a[2])
            elif w in "ms":
                reg, kw = regs[int(a[0][0])], {}
                if a[0][1:] == "a":
                    kw = {"c0": 0, "c1": 48}
                if a[0][1:] == "b":
                    kw = {"c0": 48, "c1": 96, "bank": "PR3"}
                if w == "m":
                    mm(o, reg, **kw)
                else:
                    scan(reg, *[int(x) for x in a[1:]], **kw)
            elif w == "b":
                back(regs[int(a[0])])
            elif w == "o":
                out(o, regs[int(a[0])])
            elif w == "+":
                sums[a[0]] = add(len(sums), val(a[1]), val(a[2]))
            elif w == "r":
                if a[0] == "1":
                    later.append(lay(T.RT, "RT", T.RN, "RN", T.RF, "RF"))
                else:
                    later.pop()()
            elif w == "y":
                if a[0] == "1" and o == 2:
                    op("v", [lambda: tt(T.YA[:], T.F[:, 0, :], T.F[:, 1, :], A.add)], ["F0", "F1"], ["YA"])
                if a[0] == "1" and o == 3:
                    op("v", [lambda: tt(T.YB[:], T.YA[:], T.F[:, 2, :], A.add)], ["YA", "F2"], ["YB"])
                if a[0] == "2":
                    op("v", [lambda ab=ab, h=h: V.tensor_copy(T.AR[:, 16 * h + ab:16 * h + 16:2], T.YB[:, 2 * h + ab:32:4])
                             for ab in range(2) for h in range(2)], ["YB"], ["AR"])
                    sums["Y"] = (T.AR[:], "AR")
            elif w == "f":
                finish(o, val(a[0]), int(a[1]))

    run(0, *CFG["o1"])
    run(1, *CFG["mid"])
    run(2, *CFG["mid"])
    run(3, *CFG["last"])

    for name, n in cnt.items():
        if waited.get(name, 0) < n:
            g.wait_ge(T.sem[name], n)
